import numpy as np
import ml_dtypes


def mxq(x, axis, fmt="e4m3"):
    dtype, down = {"e4m3": (ml_dtypes.float8_e4m3fn, 7), "e5m2": (ml_dtypes.float8_e5m2, 14)}[fmt]
    v = np.moveaxis(np.asarray(x, np.float32).astype(ml_dtypes.bfloat16).astype(np.float64), axis, -1)
    blocks = v.reshape(v.shape[:-1] + (-1, 32))
    amax = np.abs(blocks).max(-1, keepdims=True)
    byte = np.maximum(np.where(amax > 0, np.frexp(amax)[1] - 1 + 127, 0) - down, 1)
    scale = np.exp2(byte - 127.0)
    codes = (blocks / scale).astype(np.float32).astype(dtype).astype(np.float64)
    return np.moveaxis((codes * scale).reshape(v.shape), -1, axis)


WIDE = False


def mx_kscale(k):
    if not WIDE:
        return np.ones(k)
    levels = np.array([10, -10, 5, -5, 0])
    if k % 512:
        return np.exp2(np.random.permutation(np.resize(levels, k // 32))).repeat(32)
    a = np.empty((k // 512, 16))
    for p in range(k // 512):
        a[p, :8] = np.random.permutation(np.resize(levels, 8))
        for g in range(8):
            far = levels[np.abs(levels - a[p, g]) >= 10]
            a[p, g + 8] = far[np.random.randint(len(far))]
    return np.exp2(a.ravel()).repeat(32)


def f64(x):
    return np.asarray(x).astype(np.float64)


def striped(idx):
    return np.tile(idx.reshape(-1, 16).T, (8, 1)).astype(np.uint16)


def unstriped(offs):
    return offs[:16].T.reshape(-1).astype(np.int64)


E2M1 = np.array([0.0, 0.5, 1.0, 1.5, 2.0, 3.0, 4.0, 6.0, -0.0, -0.5, -1.0, -1.5, -2.0, -3.0, -4.0, -6.0])


def pack_weight(w, fmt):
    k, n = w.shape
    w = f64(np.asarray(w, np.float32).astype(ml_dtypes.bfloat16)).reshape(k // 32, 32, n)
    amax = np.abs(w).max(1)
    if fmt == "e4m3":
        byte = np.frexp(amax)[1] - 1 + 127 - 7
    else:
        mant, ex = np.frexp(amax / 6.0)
        byte = np.where(mant > 0.5, ex, ex - 1) + 127
    byte = np.clip(np.where(amax > 0, byte, 1), 1, 254)
    scaled = (w * np.exp2(127.0 - byte)[:, None, :]).reshape(k, n).astype(np.float32)
    by_word = np.ascontiguousarray(scaled.reshape(k // 512, 128, 4, n).transpose(0, 1, 3, 2))
    if fmt == "e4m3":
        words = by_word.astype(ml_dtypes.float8_e4m3fn).view(np.uint8)
    else:
        c = by_word.astype(ml_dtypes.float4_e2m1fn).view(np.uint8) & 0xF
        words = (c[..., 0::2] | (c[..., 1::2] << 4)).reshape(k // 512, 128, 2 * n)
    return np.ascontiguousarray(words), np.ascontiguousarray(byte.astype(np.uint8).reshape(k // 512, 16, n))


def unpack_weight(words, scales, fmt):
    g, _, n = scales.shape
    words = np.ascontiguousarray(words).reshape(g, 128, n, -1)
    if fmt == "e4m3":
        vals = words.view(ml_dtypes.float8_e4m3fn).astype(np.float64)
    else:
        nib = np.empty((g, 128, n, 4), np.uint8)
        nib[..., 0::2] = words & 0xF
        nib[..., 1::2] = words >> 4
        vals = E2M1[nib]
    vals = vals * np.repeat(np.exp2(scales.astype(np.float64) - 127.0), 8, axis=1)[..., None]
    return vals.transpose(0, 1, 3, 2).reshape(g * 512, n)


def gelu(v):
    return 0.5 * v * (1.0 + np.tanh(np.sqrt(2.0 / np.pi) * (v + 0.044715 * v**3)))


def striped8(idx):
    return np.concatenate([v.reshape(-1, 16).T for v in idx]).astype(np.uint16)


def unstriped8(offs):
    return np.stack([offs[16 * g:16 * g + 16].T.reshape(-1) for g in range(8)]).astype(np.int64)


def heads(h, wgt, idx8):
    r = np.arange(h.shape[0])
    return wgt[r // 4 % 128] * h[r[:, None], idx8[r % 512 // 64]]


def put_heads(h, wgs, idx8, t2):
    r = np.arange(h.shape[0])
    page = np.zeros((h.shape[0], t2))
    page[r[:, None], idx8[r % 512 // 64]] = wgs[r // 4 % 128] * h
    return page


K, H, N, T, S, T2, P = 512, 1024, 384, 4096, 1024, 2048, 1024

def setup_inputs():
    n = np.random.standard_normal
    s = mx_kscale(K)[:, None]
    u = mx_kscale(H)[:, None]
    d = {}
    d["tab_words"], d["tab_scales"] = pack_weight(n((K, T)) * s, "e4m3")
    d["w1"] = (n((K, H)) * 1.4 / K ** 0.5 / s * u.T).astype(np.float32)
    d["b1"] = (0.7 * n(H) * u[:, 0]).astype(np.float32)
    d["w2_words"], d["w2_scales"] = pack_weight(n((K, H)) * 1.2 / K ** 0.5 / s, "e2m1")
    d["b2"] = (0.8 * n(H)).astype(np.float32)
    d["wgs"] = np.repeat(np.random.uniform(0.5, 2.0, (8, S)), 16, axis=0).astype(np.float32)
    d["wgt"] = np.repeat(np.random.uniform(0.5, 2.0, (8, P)), 16, axis=0).astype(np.float32)
    d["stiff"] = (0.8 * n((H, P)) * u).astype(np.float32)
    d["w3"] = (n((H, N)) / H ** 0.5 / u).astype(np.float32)
    d["b3"] = (0.6 * n(N)).astype(np.float32)
    d["offs"] = striped(np.random.permutation(T)[:S])
    d["offs2"] = striped8(np.stack([np.random.permutation(T2)[:S] for _ in range(8)]))
    d["offs3"] = striped8(np.stack([np.random.permutation(T2)[:P] for _ in range(8)]))
    return d

def reference(tab_words, tab_scales, w1, b1, w2_words, w2_scales, b2, wgs, wgt, stiff, w3, b3, offs, offs2, offs3):
    v = unpack_weight(tab_words, tab_scales, "e4m3")[:, unstriped(offs)]
    lift = (mxq(f64(w1), 0, "e4m3").T @ v) + f64(b1)[:, None]
    wear = (unpack_weight(w2_words, w2_scales, "e2m1").T @ v) + f64(b2)[:, None]
    h = lift / (1.0 + np.abs(wear))
    page = put_heads(h, f64(wgs), unstriped8(offs2), T2)
    x = heads(page, f64(wgt), unstriped8(offs3))
    z = x + f64(stiff)
    y = mxq(f64(w3), 0, "e4m3").T @ mxq(z, 0, "e4m3")
    return y + f64(b3)[:, None]

@@ -1,0 +1,340 @@
+from contextlib import ExitStack
+
+import concourse.mybir as mybir
+from concourse.masks import make_identity
+
+K, H, N, T, S, T2, M = 512, 1024, 384, 4096, 1024, 2048, 1024
+FLOPS = 2 * K * H * S * 2 + 2 * H * N * M
+
+F32 = mybir.dt.float32
+BF16 = mybir.dt.bfloat16
+I32 = mybir.dt.int32
+U32 = mybir.dt.uint32
+U16 = mybir.dt.uint16
+U8 = mybir.dt.uint8
+FP8X4 = mybir.dt.float8_e4m3fn_x4
+FP4X4 = mybir.dt.float4_e2m1fn_x4
+ACT = mybir.ActivationFunctionType
+MULT = mybir.AluOpType.mult
+ADD = mybir.AluOpType.add
+
+P = 128
+PACK = 4
+HALVES = H // (P * PACK)
+GROUPS = 8
+GROUP = 16
+BANK = 512
+LOOK = 512
+
+STEPS = [(0, 0, 128), (0, 128, 128), (0, 256, 256), (0, 512, 256), (0, 768, 256),
+         (1, 0, 256), (1, 256, 256), (1, 512, 256), (1, 768, 256)]
+TAIL = [(0, 256), (256, 256), (512, 256), (768, 128), (896, 128)]
+RING = 5
+
+
+def tile_list_braille_dot_height_kernel(tc, tab_words, tab_scales, w1, b1, w2_words, w2_scales, b2, wgs, wgt,
+                                                   stiff, w3, b3, offs, offs2, offs3, out):
+    nc = tc.nc
+    with ExitStack() as ctx:
+        keep = ctx.enter_context(tc.tile_pool(name="keep", bufs=1))
+        psum = ctx.enter_context(tc.psum_pool(name="psum", bufs=1))
+
+        def alloc(name, shape, dtype, tag=None):
+            return keep.tile(shape, dtype, name=name, tag=tag or name, align_bytes=64)
+
+        banks = [psum.tile([P, BANK], F32, name="bank%d" % i) for i in range(8)]
+        wear_banks, lift_banks, turn_banks, back_banks = banks[0:2], banks[2:4], banks[4:6], banks[6:8]
+
+        idx1 = keep.tile([P, S // 16], U16, name="idx1")
+        idx2 = keep.tile([P, S // 16], U16, name="idx2")
+        idx3 = keep.tile([P, M // 16], U16, name="idx3")
+
+        tab_s = alloc("tab_s", [P, T], U8)
+        w2_s_raw = alloc("w2_s_raw", [P, H], U8)
+        nc.vector.memset(w2_s_raw[:].bitcast(I32), 0)
+        nc.vector.memset(tab_s[:].bitcast(I32), 0)
+
+        w2_w_raw = alloc("w2_w_raw", [P, 2 * H], U8)
+        nc.sync.dma_start(out=w2_w_raw[:].bitcast(I32), in_=w2_words[0].bitcast(I32))
+        tab_w = alloc("tab_w", [P, T], U32)
+        nc.sync.dma_start(out=tab_w[:].bitcast(I32), in_=tab_words[0].rearrange("p n t -> p (n t)").bitcast(I32))
+        for q in range(4):
+            nc.scalar.dma_start(out=w2_s_raw[32 * q:32 * q + 4, :].bitcast(I32), in_=w2_scales[0, 4 * q:4 * q + 4, :].bitcast(I32))
+        for q in range(4):
+            nc.scalar.dma_start(out=tab_s[32 * q:32 * q + 4, :].bitcast(I32), in_=tab_scales[0, 4 * q:4 * q + 4, :].bitcast(I32))
+        nc.sync.dma_start(idx1[:], offs)
+
+        ident = alloc("ident", [P, P], F32)
+        make_identity(nc, ident[:])
+        wgs_rows = alloc("wgs_rows", [P, P], F32)
+        nc.gpsimd.memset(wgs_rows[64:128, :], 0.0)
+        nc.sync.dma_start(out=wgs_rows[0:64, :], in_=wgs.rearrange("(g s) (c j) -> s g c j", s=GROUP, j=P)[0])
+
+        warm = alloc("warm", [P, 1], F32)
+        nc.scalar.activation(out=warm[:], in_=ident[:, 0:1], func=ACT.Abs_reciprocal_sqrt, bias=1.0)
+
+        w1_raw = [alloc("w1_raw%d" % b, [P, PACK, BANK], F32) for b in range(HALVES)]
+        w1_rows = w1.rearrange("(p j) c -> p j c", j=PACK)
+        nc.sync.dma_start(out=w1_raw[0][:], in_=w1_rows[:, :, 0:BANK])
+        b2_t = alloc("b2_t", [P, HALVES, PACK], F32)
+        nc.sync.dma_start(out=b2_t[:], in_=b2.rearrange("(b p t) -> p b t", b=HALVES, t=PACK))
+        b1_t = alloc("b1_t", [P, HALVES, PACK], F32)
+        nc.sync.dma_start(out=b1_t[:], in_=b1.rearrange("(b p t) -> p b t", b=HALVES, t=PACK))
+        nc.sync.dma_start(idx2[:], offs2)
+        nc.sync.dma_start(out=w1_raw[1][:], in_=w1_rows[:, :, BANK:2 * BANK])
+        nc.sync.dma_start(idx3[:], offs3)
+        wgt_t = alloc("wgt_t", [P, M], F32)
+        nc.sync.dma_start(out=wgt_t[:], in_=wgt)
+        w3_raw = alloc("w3_raw", [P, HALVES, PACK, N], F32)
+        nc.sync.dma_start(out=w3_raw[:].rearrange("p b j n -> p b (j n)"), in_=w3.rearrange("(b p j) n -> p b (j n)", b=HALVES, j=PACK))
+        stiff_rows = stiff.rearrange("(b p t) m -> b p t m", b=HALVES, t=PACK)
+        stiff0 = alloc("stiff0", [P, PACK, M], F32)
+        nc.sync.dma_start(out=stiff0[:], in_=stiff_rows[0])
+        b3_t = alloc("b3_t", [P, N // P], F32)
+        with nc.allow_non_contiguous_dma(reason="one bias value a partition"):
+            nc.sync.dma_start(out=b3_t[:], in_=b3.rearrange("(c p) -> p c", p=P))
+
+        w2_w = alloc("w2_w", [P, HALVES, 2 * BANK], U8)
+        w2_s = alloc("w2_s", [P, HALVES, BANK], U8)
+        for b in range(HALVES):
+            nc.vector.tensor_copy(out=w2_w[:, b, :].rearrange("p (t q e) -> p t q e", t=PACK, e=2),
+                                  in_=w2_w_raw[:, 2 * BANK * b:2 * BANK * (b + 1)].rearrange("p (q t e) -> p t q e", t=PACK, e=2))
+            nc.vector.tensor_copy(out=w2_s[:, b, :].rearrange("p (t q) -> p t q", t=PACK),
+                                  in_=w2_s_raw[:, BANK * b:BANK * (b + 1)].rearrange("p (q t) -> p t q", t=PACK))
+
+        nc.tensor.transpose(back_banks[1][:, 0:P], wgs_rows[:], ident[:])
+        inv_wgs = alloc("inv_wgs", [P, GROUPS * (S // P)], F32)
+        nc.vector.reciprocal(out=inv_wgs[:], in_=back_banks[1][:, 0:GROUPS * (S // P)])
+
+        pages = [alloc("page%d" % t, [P, T2], F32) for t in range(PACK)]
+        for t in range(PACK):
+            nc.vector.memset(pages[t][:], 0.0)
+
+        v_w = [alloc("v_w%d" % h, [P, LOOK], U32) for h in range(S // LOOK)]
+        v_s = [alloc("v_s%d" % h, [P, LOOK], U8) for h in range(S // LOOK)]
+
+        def look_up(h):
+            cols = idx1[:, h * LOOK // 16:(h + 1) * LOOK // 16]
+            nc.vector.tensor_copy(out=v_w[h][:], in_=tab_w[:].indirect(cols))
+            nc.vector.tensor_copy(out=v_s[h][:], in_=tab_s[:].indirect(cols))
+
+        w1_g = [alloc("w1_g%d" % b, [P, PACK * BANK], BF16) for b in range(HALVES)]
+        w1_w = [alloc("w1_w%d" % b, [P, BANK], U32) for b in range(HALVES)]
+        w1_s = [alloc("w1_s%d" % b, [P, BANK], U8) for b in range(HALVES)]
+
+        def round_w1(copy, b, m0, m1):
+            copy(out=w1_g[b][:].rearrange("p (t m j) -> p m j t", t=PACK, j=PACK)[:, m0:m1],
+                 in_=w1_raw[b][:].rearrange("p j (m t) -> p m j t", t=PACK)[:, m0:m1])
+
+        def quantize(words, scales, values):
+            nc.vector.quantize_mx(out=words.bitcast(FP8X4), scales=scales, in_=values)
+
+        look_up(0)
+        round_w1(nc.vector.tensor_copy, 0, 0, P)
+        quantize(w1_w[0][:], w1_s[0][:], w1_g[0][:])
+        look_up(1)
+
+        mags = [alloc("mag%d" % i, [P, PACK, 256], F32) for i in range(2)]
+        roots = [alloc("root%d" % i, [P, PACK, P], F32) for i in range(2)]
+        damp = {}
+        lift = {}
+
+        def place(banks2, t, width):
+            per = BANK // width
+            return banks2[t // per][:, (t % per) * width:(t % per + 1) * width]
+
+        def moving(j0, width):
+            h, c = divmod(j0, LOOK)
+            return v_w[h][:, c:c + width].bitcast(FP8X4), v_s[h][:, c:c + width]
+
+        def wear_products(u):
+            b, j0, width = STEPS[u]
+            rhs, rhs_s = moving(j0, width)
+            for t in range(PACK):
+                nc.tensor.matmul_mx(out=place(wear_banks, t, width), lhsT=w2_w[:, b, 2 * P * t:2 * P * (t + 1)].bitcast(FP4X4),
+                                    lhsT_scale=w2_s[:, b, P * t:P * (t + 1)], rhs=rhs, rhs_scale=rhs_s, start=True, stop=True)
+
+        def lift_products(u):
+            b, j0, width = STEPS[u]
+            rhs, rhs_s = moving(j0, width)
+            for t in range(PACK):
+                nc.tensor.matmul_mx(out=place(lift_banks, t, width), lhsT=w1_w[b][:, P * t:P * (t + 1)].bitcast(FP8X4),
+                                    lhsT_scale=w1_s[b][:, P * t:P * (t + 1)], rhs=rhs, rhs_scale=rhs_s, start=True, stop=True)
+
+        def magnitudes(u):
+            b, j0, width = STEPS[u]
+            for t in range(PACK):
+                nc.scalar.activation(out=mags[u % 2][:, t, 0:width], in_=place(wear_banks, t, width), func=ACT.Abs,
+                                     bias=b2_t[:, b, t:t + 1])
+
+        def turn(u, c):
+            bank = turn_banks[(STEPS[u][1] // P + c) % 2]
+            for t in range(PACK):
+                nc.tensor.transpose(bank[:, P * t:P * (t + 1)], mags[u % 2][:, t, P * c:P * (c + 1)], ident[:])
+
+        def inverse_roots(u, c):
+            chunk = STEPS[u][1] // P + c
+            bank = turn_banks[chunk % 2][:].rearrange("j (t p) -> j t p", t=PACK)
+            for g in range(GROUPS):
+                col = inv_wgs[:, g * (S // P) + chunk:g * (S // P) + chunk + 1]
+                nc.scalar.activation(out=roots[chunk % 2][:, :, GROUP * g:GROUP * (g + 1)], in_=bank[:, :, GROUP * g:GROUP * (g + 1)],
+                                     func=ACT.Abs_reciprocal_sqrt, bias=col, scale=col)
+
+        def turn_back(u, c):
+            chunk = STEPS[u][1] // P + c
+            for t in range(PACK):
+                nc.tensor.transpose(back_banks[chunk % 2][:, P * t:P * (t + 1)], roots[chunk % 2][:, t, :], ident[:])
+
+        def squares(u, c):
+            chunk = STEPS[u][1] // P + c
+            if c == 0:
+                damp[u] = alloc("damp%d" % u, [P, PACK, STEPS[u][2]], F32, tag="damp%d" % (u % RING))
+            nc.scalar.activation(out=damp[u][:, :, P * c:P * (c + 1)], in_=back_banks[chunk % 2][:].rearrange("p (t j) -> p t j", t=PACK),
+                                 func=ACT.Square)
+
+        def lifts(u):
+            b, j0, width = STEPS[u]
+            lift[u] = alloc("lift%d" % u, [P, PACK, width], F32, tag="lift%d" % (u % RING))
+            for t in range(PACK):
+                nc.scalar.activation(out=lift[u][:, t, :], in_=place(lift_banks, t, width), func=ACT.Identity, bias=b1_t[:, b, t:t + 1])
+
+        def put(u):
+            b, j0, width = STEPS[u]
+            cols = idx2[:, j0 // 16:(j0 + width) // 16]
+            for t in range(PACK):
+                nc.vector.tensor_tensor(pages[t][:].indirect(cols), lift[u][:, t, :], damp[u][:, t, :], MULT)
+
+        x = alloc("x", [P, PACK, M], F32)
+
+        def pick(t, m0, width):
+            nc.vector.tensor_tensor(x[:, t, m0:m0 + width], pages[t][:].indirect(idx3[:, m0 // 16:(m0 + width) // 16]),
+                                    wgt_t[:, m0:m0 + width], MULT)
+
+        stiff1 = []
+
+        wear_products(0)
+        magnitudes(0)
+        for u in range(len(STEPS)):
+            chunks = range(STEPS[u][2] // P)
+            for c in chunks:
+                turn(u, c)
+            lift_products(u)
+            if u + 1 < len(STEPS):
+                wear_products(u + 1)
+            for c in chunks:
+                inverse_roots(u, c)
+                turn_back(u, c)
+            lifts(u)
+            if u + 1 < len(STEPS) and u > 0:
+                magnitudes(u + 1)
+            for c in chunks:
+                squares(u, c)
+            if u == 0:
+                magnitudes(1)
+            put(u)
+            if u in (1, 2):
+                for m0 in range(64 * (u - 1), 64 * u, 32):
+                    round_w1(nc.scalar.copy, 1, m0, m0 + 32)
+            if u == 2:
+                quantize(w1_w[1][:], w1_s[1][:], w1_g[1][:])
+                for h in range(2):
+                    half = alloc("stiff1_%d" % h, [P, PACK, BANK], F32, tag="w1_raw%d" % h)
+                    nc.sync.dma_start(out=half[:], in_=stiff_rows[1][:, :, BANK * h:BANK * (h + 1)])
+                    stiff1.append(half)
+            if u == 4:
+                for t in range(PACK):
+                    pick(t, 0, M)
+
+        z_g = alloc("z_g", [P, M * PACK], BF16)
+        z_w = [alloc("z_w%d" % b, [P, M], U32) for b in range(HALVES)]
+        z_s = [alloc("z_s%d" % b, [P, M], U8) for b in range(HALVES)]
+        z_t = [alloc("z_t%d" % i, [P, PACK * P], BF16) for i in range(2)]
+        sum_banks = turn_banks + back_banks
+
+        def sums(c):
+            bank = sum_banks[c % 4]
+            for t in range(PACK):
+                nc.tensor.matmul(bank[:, P * t:P * (t + 1)], lhsT=stiff0[:, t, P * c:P * (c + 1)], rhs=ident[:], start=True, stop=False,
+                                 is_transpose=True)
+                nc.tensor.matmul(bank[:, P * t:P * (t + 1)], lhsT=x[:, t, P * c:P * (c + 1)], rhs=ident[:], start=False, stop=True,
+                                 is_transpose=True)
+
+        def round_sums(c):
+            nc.scalar.copy(out=z_t[c % 2][:].rearrange("m (u p e) -> m u p e", u=2, e=2),
+                           in_=sum_banks[c % 4][:].rearrange("m (u e p) -> m u p e", u=2, e=2))
+
+        def words_back(c):
+            words = z_t[c % 2][:].bitcast(F32)
+            bank = wear_banks[c // 2 % 2]
+            for u in range(2):
+                o = (c % 2) * 2 * P + u * P
+                nc.tensor.transpose(bank[:, o:o + P], words[:, P * u:P * (u + 1)], ident[:])
+
+        def weave(pair):
+            words = z_g[:].bitcast(F32)[:, 4 * P * pair:4 * P * (pair + 1)]
+            nc.scalar.copy(out=words.rearrange("p (c m u) -> p c m u", c=2, u=2),
+                           in_=wear_banks[pair % 2][:].rearrange("p (c u m) -> p c m u", c=2, u=2))
+
+        def quantize_z(b, m0, width):
+            quantize(z_w[b][:, m0:m0 + width], z_s[b][:, m0:m0 + width], z_g[:, PACK * m0:PACK * (m0 + width)])
+
+        sums(0)
+        sums(1)
+        for c in range(M // P):
+            if c + 2 < M // P:
+                sums(c + 2)
+            round_sums(c)
+            words_back(c)
+            if c % 2 == 0 and c > 0:
+                weave(c // 2 - 1)
+        weave(M // P // 2 - 1)
+        for h in range(2):
+            quantize_z(0, BANK * h, BANK)
+
+        w3_g = alloc("w3_g", [P, HALVES, N * PACK], BF16)
+        w3_w = alloc("w3_w", [P, HALVES * N], U32)
+        w3_s = alloc("w3_s", [P, HALVES * N], U8)
+        for b in range(HALVES):
+            for c in range(N // P):
+                nc.scalar.copy(out=w3_g[:, b, PACK * P * c:PACK * P * (c + 1)].rearrange("p (c i j) -> p c j i", i=4, j=PACK),
+                               in_=w3_raw[:, b, :, P * c:P * (c + 1)].rearrange("p j (c i) -> p c j i", i=4))
+        w3_flat = w3_g[:].rearrange("p b n -> p (b n)")
+        quantize(w3_w[:, 0:512], w3_s[:, 0:512], w3_flat[:, 0:2048])
+        quantize(w3_w[:, 512:768], w3_s[:, 512:768], w3_flat[:, 2048:3072])
+
+        out_rows = out.rearrange("(c p) m -> p c m", p=P)
+
+        def add_stiff(m0, width):
+            h, c = divmod(m0, BANK)
+            nc.vector.tensor_tensor(z_g[:, PACK * m0:PACK * (m0 + width)].rearrange("p (c i t) -> p c t i", i=4, t=PACK),
+                                    x[:, :, m0:m0 + width].rearrange("p t (c i) -> p c t i", i=4),
+                                    stiff1[h][:, :, c:c + width].rearrange("p t (c i) -> p c t i", i=4), ADD)
+
+        def last_product(i):
+            m0, width = TAIL[i]
+            two = banks[(2 * i + 2) % 8:(2 * i + 2) % 8 + 2]
+            result = alloc("result%d" % i, [P, N // P, width], F32, tag="lift%d" % (i % RING))
+            for c in range(N // P):
+                for b in range(HALVES):
+                    cols = slice(N * b + P * c, N * b + P * (c + 1))
+                    nc.tensor.matmul_mx(out=place(two, c, width), lhsT=w3_w[:, cols].bitcast(FP8X4), lhsT_scale=w3_s[:, cols],
+                                        rhs=z_w[b][:, m0:m0 + width].bitcast(FP8X4), rhs_scale=z_s[b][:, m0:m0 + width],
+                                        start=(b == 0), stop=(b == HALVES - 1))
+            for c in range(N // P):
+                nc.scalar.activation(out=result[:, c, :], in_=place(two, c, width), func=ACT.Identity, bias=b3_t[:, c:c + 1])
+            nc.sync.dma_start(out=out_rows[:, :, m0:m0 + width], in_=result[:])
+
+        for t in range(PACK):
+            pick(t, *TAIL[0])
+        for i in range(len(TAIL)):
+            ahead = TAIL[i + 1] if i + 1 < len(TAIL) else None
+            if ahead:
+                pick(0, *ahead)
+            add_stiff(*TAIL[i])
+            if ahead:
+                pick(1, *ahead)
+            quantize_z(1, *TAIL[i])
+            if ahead:
+                pick(2, *ahead)
+                pick(3, *ahead)
+            last_product(i)

@@ -36,6 +36,7 @@ def tile_list_braille_dot_height_kernel(tc, tab_words, tab_scales, w1, b1, w2_wo
                                                    stiff, w3, b3, offs, offs2, offs3, out):
     nc = tc.nc
     with ExitStack() as ctx:
+        lists = ctx.enter_context(tc.tile_pool(name="lists", bufs=1))
         keep = ctx.enter_context(tc.tile_pool(name="keep", bufs=1))
         psum = ctx.enter_context(tc.psum_pool(name="psum", bufs=1))
 
@@ -45,43 +46,38 @@ def tile_list_braille_dot_height_kernel(tc, tab_words, tab_scales, w1, b1, w2_wo
         banks = [psum.tile([P, BANK], F32, name="bank%d" % i) for i in range(8)]
         wear_banks, lift_banks, turn_banks, back_banks = banks[0:2], banks[2:4], banks[4:6], banks[6:8]
 
-        idx1 = keep.tile([P, S // 16], U16, name="idx1")
-        idx2 = keep.tile([P, S // 16], U16, name="idx2")
-        idx3 = keep.tile([P, M // 16], U16, name="idx3")
+        idx1 = lists.tile([P, S // 16], U16, name="idx1")
+        idx2 = lists.tile([P, S // 16], U16, name="idx2")
+        idx3 = lists.tile([P, M // 16], U16, name="idx3")
 
         tab_s = alloc("tab_s", [P, T], U8)
-        w2_s_raw = alloc("w2_s_raw", [P, H], U8)
-        nc.vector.memset(w2_s_raw[:].bitcast(I32), 0)
+        w2_s = alloc("w2_s", [P, H], U8)
         nc.vector.memset(tab_s[:].bitcast(I32), 0)
+        nc.vector.memset(w2_s[:].bitcast(I32), 0)
 
-        w2_w_raw = alloc("w2_w_raw", [P, 2 * H], U8)
-        nc.sync.dma_start(out=w2_w_raw[:].bitcast(I32), in_=w2_words[0].bitcast(I32))
         tab_w = alloc("tab_w", [P, T], U32)
-        nc.sync.dma_start(out=tab_w[:].bitcast(I32), in_=tab_words[0].rearrange("p n t -> p (n t)").bitcast(I32))
-        for q in range(4):
-            nc.scalar.dma_start(out=w2_s_raw[32 * q:32 * q + 4, :].bitcast(I32), in_=w2_scales[0, 4 * q:4 * q + 4, :].bitcast(I32))
-        for q in range(4):
-            nc.scalar.dma_start(out=tab_s[32 * q:32 * q + 4, :].bitcast(I32), in_=tab_scales[0, 4 * q:4 * q + 4, :].bitcast(I32))
-        nc.sync.dma_start(idx1[:], offs)
-
-        ident = alloc("ident", [P, P], F32)
-        make_identity(nc, ident[:])
-        wgs_rows = alloc("wgs_rows", [P, P], F32)
-        nc.gpsimd.memset(wgs_rows[64:128, :], 0.0)
-        nc.sync.dma_start(out=wgs_rows[0:64, :], in_=wgs.rearrange("(g s) (c j) -> s g c j", s=GROUP, j=P)[0])
-
-        warm = alloc("warm", [P, 1], F32)
-        nc.scalar.activation(out=warm[:], in_=ident[:, 0:1], func=ACT.Abs_reciprocal_sqrt, bias=1.0)
-
-        w1_raw = [alloc("w1_raw%d" % b, [P, PACK, BANK], F32) for b in range(HALVES)]
+        tab_src = tab_words[0].rearrange("p n t -> p (n t)").bitcast(I32)
+        w2_src = w2_words[0].bitcast(I32)
+        w2_w = [alloc("w2_w%d" % b, [P, 2 * BANK], U8) for b in range(HALVES)]
         w1_rows = w1.rearrange("(p j) c -> p j c", j=PACK)
-        nc.sync.dma_start(out=w1_raw[0][:], in_=w1_rows[:, :, 0:BANK])
-        b2_t = alloc("b2_t", [P, HALVES, PACK], F32)
-        nc.sync.dma_start(out=b2_t[:], in_=b2.rearrange("(b p t) -> p b t", b=HALVES, t=PACK))
+        w1_raw = [[alloc("w1_raw0_%d" % h, [P, PACK, BANK // 2], F32) for h in range(2)]]
+
+        nc.sync.dma_start(idx1[:], offs)
+        nc.sync.dma_start(out=tab_w[:].bitcast(I32)[:, 0:T // 2], in_=tab_src[:, 0:T // 2])
+        for q in range(4):
+            nc.sync.dma_start(out=tab_s[32 * q:32 * q + 4, :].bitcast(I32), in_=tab_scales[0, 4 * q:4 * q + 4, :].bitcast(I32))
+        nc.sync.dma_start(out=w2_w[0][:].bitcast(I32), in_=w2_src[:, 0:BANK // 2])
+        nc.sync.dma_start(out=tab_w[:].bitcast(I32)[:, T // 2:T], in_=tab_src[:, T // 2:T])
+        for q in range(4):
+            nc.sync.dma_start(out=w2_s[32 * q:32 * q + 4, :].bitcast(I32), in_=w2_scales[0, 4 * q:4 * q + 4, :].bitcast(I32))
+        for h in range(2):
+            nc.sync.dma_start(out=w1_raw[0][h][:], in_=w1_rows[:, :, h * BANK // 2:(h + 1) * BANK // 2])
+        nc.sync.dma_start(idx2[:], offs2)
         b1_t = alloc("b1_t", [P, HALVES, PACK], F32)
         nc.sync.dma_start(out=b1_t[:], in_=b1.rearrange("(b p t) -> p b t", b=HALVES, t=PACK))
-        nc.sync.dma_start(idx2[:], offs2)
-        nc.sync.dma_start(out=w1_raw[1][:], in_=w1_rows[:, :, BANK:2 * BANK])
+        nc.sync.dma_start(out=w2_w[1][:].bitcast(I32), in_=w2_src[:, BANK // 2:BANK])
+        w1_raw.append([alloc("w1_raw1", [P, PACK, BANK], F32)])
+        nc.sync.dma_start(out=w1_raw[1][0][:], in_=w1_rows[:, :, BANK:2 * BANK])
         nc.sync.dma_start(idx3[:], offs3)
         wgt_t = alloc("wgt_t", [P, M], F32)
         nc.sync.dma_start(out=wgt_t[:], in_=wgt)
@@ -94,65 +90,85 @@ def tile_list_braille_dot_height_kernel(tc, tab_words, tab_scales, w1, b1, w2_wo
         with nc.allow_non_contiguous_dma(reason="one bias value a partition"):
             nc.sync.dma_start(out=b3_t[:], in_=b3.rearrange("(c p) -> p c", p=P))
 
-        w2_w = alloc("w2_w", [P, HALVES, 2 * BANK], U8)
-        w2_s = alloc("w2_s", [P, HALVES, BANK], U8)
-        for b in range(HALVES):
-            nc.vector.tensor_copy(out=w2_w[:, b, :].rearrange("p (t q e) -> p t q e", t=PACK, e=2),
-                                  in_=w2_w_raw[:, 2 * BANK * b:2 * BANK * (b + 1)].rearrange("p (q t e) -> p t q e", t=PACK, e=2))
-            nc.vector.tensor_copy(out=w2_s[:, b, :].rearrange("p (t q) -> p t q", t=PACK),
-                                  in_=w2_s_raw[:, BANK * b:BANK * (b + 1)].rearrange("p (q t) -> p t q", t=PACK))
+        CHUNKS = S // P
+        W_ROWS = GROUPS * CHUNKS
+        rows = alloc("rows", [P, P], F32)
+        nc.gpsimd.memset(rows[:], 0.0)
+        nc.gpsimd.dma_start(out=rows[0:W_ROWS, :], in_=wgs.rearrange("(g s) (c j) -> s g c j", s=GROUP, j=P)[0])
+        nc.gpsimd.dma_start(out=rows[W_ROWS:W_ROWS + H // P, :], in_=b2.rearrange("(c p) -> c p", p=P))
+        ident = alloc("ident", [P, P], F32)
+        make_identity(nc, ident[:])
 
-        nc.tensor.transpose(back_banks[1][:, 0:P], wgs_rows[:], ident[:])
-        inv_wgs = alloc("inv_wgs", [P, GROUPS * (S // P)], F32)
-        nc.vector.reciprocal(out=inv_wgs[:], in_=back_banks[1][:, 0:GROUPS * (S // P)])
+        warm = alloc("warm", [P, 1], F32)
+        nc.scalar.activation(out=warm[:], in_=ident[:, 0:1], func=ACT.Abs_reciprocal_sqrt, bias=1.0)
 
         pages = [alloc("page%d" % t, [P, T2], F32) for t in range(PACK)]
         for t in range(PACK):
-            nc.vector.memset(pages[t][:], 0.0)
+            nc.vector.memset(pages[t][:].bitcast(I32), 0)
 
+        nc.tensor.transpose(back_banks[1][:, 0:P], rows[:], ident[:])
+        inv_wgs = alloc("inv_wgs", [P, W_ROWS], F32)
+        b2_t = alloc("b2_t", [P, H // P], F32)
+        nc.scalar.copy(out=b2_t[:], in_=back_banks[1][:, W_ROWS:W_ROWS + H // P])
+        nc.vector.reciprocal(out=inv_wgs[:], in_=back_banks[1][:, 0:W_ROWS])
+
+        v_s = alloc("v_s", [P, S], U8)
+        nc.vector.tensor_copy(out=v_s[:], in_=tab_s[:].indirect(idx1[:]))
         v_w = [alloc("v_w%d" % h, [P, LOOK], U32) for h in range(S // LOOK)]
-        v_s = [alloc("v_s%d" % h, [P, LOOK], U8) for h in range(S // LOOK)]
+        for h in range(S // LOOK):
+            nc.vector.tensor_copy(out=v_w[h][:], in_=tab_w[:].indirect(idx1[:, h * LOOK // 16:(h + 1) * LOOK // 16]))
 
-        def look_up(h):
-            cols = idx1[:, h * LOOK // 16:(h + 1) * LOOK // 16]
-            nc.vector.tensor_copy(out=v_w[h][:], in_=tab_w[:].indirect(cols))
-            nc.vector.tensor_copy(out=v_s[h][:], in_=tab_s[:].indirect(cols))
-
-        w1_g = [alloc("w1_g%d" % b, [P, PACK * BANK], BF16) for b in range(HALVES)]
+        w1_g = [alloc("w1_g0", [P, PACK * BANK], BF16)]
         w1_w = [alloc("w1_w%d" % b, [P, BANK], U32) for b in range(HALVES)]
         w1_s = [alloc("w1_s%d" % b, [P, BANK], U8) for b in range(HALVES)]
 
-        def round_w1(copy, b, m0, m1):
-            copy(out=w1_g[b][:].rearrange("p (t m j) -> p m j t", t=PACK, j=PACK)[:, m0:m1],
-                 in_=w1_raw[b][:].rearrange("p j (m t) -> p m j t", t=PACK)[:, m0:m1])
+        def round_w1(copy, b, src, m0, count):
+            copy(out=w1_g[b][:].rearrange("p (t m j) -> p m t j", t=PACK, j=PACK)[:, m0:m0 + count],
+                 in_=src.rearrange("p j (m t) -> p m t j", t=PACK))
 
         def quantize(words, scales, values):
             nc.vector.quantize_mx(out=words.bitcast(FP8X4), scales=scales, in_=values)
 
-        look_up(0)
-        round_w1(nc.vector.tensor_copy, 0, 0, P)
-        quantize(w1_w[0][:], w1_s[0][:], w1_g[0][:])
-        look_up(1)
+        for h in range(2):
+            round_w1(nc.vector.tensor_copy, 0, w1_raw[0][h][:], h * P // 2, P // 2)
+        for h in range(2):
+            cols = slice(h * BANK // 2, (h + 1) * BANK // 2)
+            quantize(w1_w[0][:, cols], w1_s[0][:, cols], w1_g[0][:, h * 2 * BANK:(h + 1) * 2 * BANK])
+
+        stiff1 = [alloc("stiff1_%d" % h, [P, PACK, BANK], F32, tag="w1_raw0_%d" % h) for h in range(2)]
+        for h in range(2):
+            nc.sync.dma_start(out=stiff1[h][:], in_=stiff_rows[1][:, :, BANK * h:BANK * (h + 1)])
 
         mags = [alloc("mag%d" % i, [P, PACK, 256], F32) for i in range(2)]
-        roots = [alloc("root%d" % i, [P, PACK, P], F32) for i in range(2)]
+        root_pair = [alloc("root%d" % i, [P, PACK, P], F32) for i in range(2)]
+        root_last = alloc("root_last", [P, PACK, P], F32)
+
+        def root(u, k):
+            chunk = STEPS[u][1] // P + k
+            return root_last if (STEPS[u][0], chunk) == (0, CHUNKS - 1) else root_pair[chunk % 2]
+
         damp = {}
         lift = {}
 
-        def place(banks2, t, width):
-            per = BANK // width
-            return banks2[t // per][:, (t % per) * width:(t % per + 1) * width]
+        def place(banks2, i, width):
+            return banks2[i // 2][:, (i % 2) * width:(i % 2 + 1) * width]
+
+        def block(banks2, u, k, i):
+            per = PACK * (STEPS[u][2] // P) // 2
+            h, c = divmod(PACK * k + i, per)
+            return banks2[h][:, P * c:P * (c + 1)]
 
         def moving(j0, width):
             h, c = divmod(j0, LOOK)
-            return v_w[h][:, c:c + width].bitcast(FP8X4), v_s[h][:, c:c + width]
+            return v_w[h][:, c:c + width].bitcast(FP8X4), v_s[:, j0:j0 + width]
 
         def wear_products(u):
             b, j0, width = STEPS[u]
             rhs, rhs_s = moving(j0, width)
-            for t in range(PACK):
-                nc.tensor.matmul_mx(out=place(wear_banks, t, width), lhsT=w2_w[:, b, 2 * P * t:2 * P * (t + 1)].bitcast(FP4X4),
-                                    lhsT_scale=w2_s[:, b, P * t:P * (t + 1)], rhs=rhs, rhs_scale=rhs_s, start=True, stop=True)
+            for c in range(PACK):
+                nc.tensor.matmul_mx(out=place(wear_banks, c, width), lhsT=w2_w[b][:, 2 * P * c:2 * P * (c + 1)].bitcast(FP4X4),
+                                    lhsT_scale=w2_s[:, BANK * b + P * c:BANK * b + P * (c + 1)], rhs=rhs, rhs_scale=rhs_s,
+                                    start=True, stop=True)
 
         def lift_products(u):
             b, j0, width = STEPS[u]
@@ -163,34 +179,37 @@ def tile_list_braille_dot_height_kernel(tc, tab_words, tab_scales, w1, b1, w2_wo
 
         def magnitudes(u):
             b, j0, width = STEPS[u]
-            for t in range(PACK):
-                nc.scalar.activation(out=mags[u % 2][:, t, 0:width], in_=place(wear_banks, t, width), func=ACT.Abs,
-                                     bias=b2_t[:, b, t:t + 1])
+            for c in range(PACK):
+                nc.scalar.activation(out=mags[u % 2][:, c, 0:width], in_=place(wear_banks, c, width), func=ACT.Abs,
+                                     bias=b2_t[:, PACK * b + c:PACK * b + c + 1])
 
-        def turn(u, c):
-            bank = turn_banks[(STEPS[u][1] // P + c) % 2]
-            for t in range(PACK):
-                nc.tensor.transpose(bank[:, P * t:P * (t + 1)], mags[u % 2][:, t, P * c:P * (c + 1)], ident[:])
+        def turn(u, k):
+            for c in range(PACK):
+                nc.tensor.transpose(block(turn_banks, u, k, c), mags[u % 2][:, c, P * k:P * (k + 1)], ident[:])
 
-        def inverse_roots(u, c):
-            chunk = STEPS[u][1] // P + c
-            bank = turn_banks[chunk % 2][:].rearrange("j (t p) -> j t p", t=PACK)
+        def inverse_roots(u, k):
+            chunk = STEPS[u][1] // P + k
             for g in range(GROUPS):
-                col = inv_wgs[:, g * (S // P) + chunk:g * (S // P) + chunk + 1]
-                nc.scalar.activation(out=roots[chunk % 2][:, :, GROUP * g:GROUP * (g + 1)], in_=bank[:, :, GROUP * g:GROUP * (g + 1)],
+                col = inv_wgs[:, g * CHUNKS + chunk:g * CHUNKS + chunk + 1]
+                run = block(turn_banks, u, k, g // 2)[:, 64 * (g % 2):64 * (g % 2 + 1)]
+                nc.scalar.activation(out=root(u, k)[:, :, GROUP * g:GROUP * (g + 1)], in_=run.rearrange("j (s t) -> j t s", t=PACK),
                                      func=ACT.Abs_reciprocal_sqrt, bias=col, scale=col)
 
-        def turn_back(u, c):
-            chunk = STEPS[u][1] // P + c
+        def turn_back(u, k):
             for t in range(PACK):
-                nc.tensor.transpose(back_banks[chunk % 2][:, P * t:P * (t + 1)], roots[chunk % 2][:, t, :], ident[:])
+                nc.tensor.transpose(block(back_banks, u, k, t), root(u, k)[:, t, :], ident[:])
 
-        def squares(u, c):
-            chunk = STEPS[u][1] // P + c
-            if c == 0:
-                damp[u] = alloc("damp%d" % u, [P, PACK, STEPS[u][2]], F32, tag="damp%d" % (u % RING))
-            nc.scalar.activation(out=damp[u][:, :, P * c:P * (c + 1)], in_=back_banks[chunk % 2][:].rearrange("p (t j) -> p t j", t=PACK),
-                                 func=ACT.Square)
+        def squares(u, k):
+            width = STEPS[u][2]
+            if k == 0:
+                damp[u] = alloc("damp%d" % u, [P, PACK, width], F32, tag="damp%d" % (u % RING))
+            if width == P:
+                for h in range(2):
+                    nc.scalar.activation(out=damp[u][:, 2 * h:2 * h + 2, :], in_=back_banks[h][:, 0:2 * P].rearrange("p (t j) -> p t j", t=2),
+                                         func=ACT.Square)
+            else:
+                nc.scalar.activation(out=damp[u][:, :, P * k:P * (k + 1)], in_=back_banks[k][:].rearrange("p (t j) -> p t j", t=PACK),
+                                     func=ACT.Square)
 
         def lifts(u):
             b, j0, width = STEPS[u]
@@ -198,66 +217,81 @@ def tile_list_braille_dot_height_kernel(tc, tab_words, tab_scales, w1, b1, w2_wo
             for t in range(PACK):
                 nc.scalar.activation(out=lift[u][:, t, :], in_=place(lift_banks, t, width), func=ACT.Identity, bias=b1_t[:, b, t:t + 1])
 
-        def put(u):
-            b, j0, width = STEPS[u]
+        def put(u, c0, width):
+            j0 = STEPS[u][1] + c0
             cols = idx2[:, j0 // 16:(j0 + width) // 16]
             for t in range(PACK):
-                nc.vector.tensor_tensor(pages[t][:].indirect(cols), lift[u][:, t, :], damp[u][:, t, :], MULT)
+                nc.vector.tensor_tensor(pages[t][:].indirect(cols), lift[u][:, t, c0:c0 + width], damp[u][:, t, c0:c0 + width], MULT)
 
-        x = alloc("x", [P, PACK, M], F32)
+        def pick(dst, t, m0, width):
+            nc.vector.tensor_tensor(dst, pages[t][:].indirect(idx3[:, m0 // 16:(m0 + width) // 16]), wgt_t[:, m0:m0 + width], MULT)
 
-        def pick(t, m0, width):
-            nc.vector.tensor_tensor(x[:, t, m0:m0 + width], pages[t][:].indirect(idx3[:, m0 // 16:(m0 + width) // 16]),
-                                    wgt_t[:, m0:m0 + width], MULT)
+        w3_w = alloc("w3_w", [P, HALVES * N], U32)
+        w3_s = alloc("w3_s", [P, HALVES * N], U8)
+        x_first = []
 
-        stiff1 = []
+        def between_halves():
+            w1_g.append(alloc("w1_g1", [P, PACK * BANK], BF16, tag="root_last"))
+            for m0 in range(0, P, 32):
+                round_w1(nc.scalar.copy, 1, w1_raw[1][0][:, :, PACK * m0:PACK * (m0 + 32)], m0, 32)
+            quantize(w1_w[1][:], w1_s[1][:], w1_g[1][:])
+            for t in range(PACK):
+                x_first.append(alloc("x_first%d" % t, [P, M], F32, tag="root_last" if t == 0 else None))
+                pick(x_first[t][:], t, 0, M)
 
+        FIRST = [u for u in range(len(STEPS)) if STEPS[u][0] == 0]
+        LATE = [len(FIRST), len(FIRST) + 1]
         wear_products(0)
         magnitudes(0)
         for u in range(len(STEPS)):
-            chunks = range(STEPS[u][2] // P)
-            for c in chunks:
-                turn(u, c)
-            lift_products(u)
-            if u + 1 < len(STEPS):
-                wear_products(u + 1)
-            for c in chunks:
-                inverse_roots(u, c)
-                turn_back(u, c)
-            lifts(u)
-            if u + 1 < len(STEPS) and u > 0:
-                magnitudes(u + 1)
-            for c in chunks:
-                squares(u, c)
-            if u == 0:
-                magnitudes(1)
-            put(u)
-            if u in (1, 2):
-                for m0 in range(64 * (u - 1), 64 * u, 32):
-                    round_w1(nc.scalar.copy, 1, m0, m0 + 32)
-            if u == 2:
-                quantize(w1_w[1][:], w1_s[1][:], w1_g[1][:])
-                for h in range(2):
-                    half = alloc("stiff1_%d" % h, [P, PACK, BANK], F32, tag="w1_raw%d" % h)
-                    nc.sync.dma_start(out=half[:], in_=stiff_rows[1][:, :, BANK * h:BANK * (h + 1)])
-                    stiff1.append(half)
-            if u == 4:
-                for t in range(PACK):
-                    pick(t, 0, M)
+            width = STEPS[u][2]
+            last = width // P - 1
+            for k in range(last + 1):
+                turn(u, k)
+            if u not in LATE:
+                lift_products(u)
+            for k in range(last + 1):
+                inverse_roots(u, k)
+                turn_back(u, k)
+                if k == 0 and u not in LATE:
+                    lifts(u)
+                if k == last and u + 1 < len(STEPS):
+                    wear_products(u + 1)
+                    magnitudes(u + 1)
+                squares(u, k)
+                if u in FIRST:
+                    put(u, P * k, P)
+            if u == FIRST[-1]:
+                between_halves()
+            elif u == LATE[-1]:
+                for v in LATE:
+                    lift_products(v)
+                    lifts(v)
+                    put(v, 0, width)
+            elif u > LATE[-1]:
+                put(u, 0, width)
 
-        z_g = alloc("z_g", [P, M * PACK], BF16)
+        w3_g = alloc("w3_g", [P, HALVES, N * PACK], BF16, tag="w1_raw1")
+        for b in range(HALVES):
+            for c in range(N // P):
+                nc.scalar.copy(out=w3_g[:, b, PACK * P * c:PACK * P * (c + 1)].rearrange("p (n j) -> p n j", j=PACK),
+                               in_=w3_raw[:, b, :, P * c:P * (c + 1)].rearrange("p j n -> p n j"))
+        w3_flat = w3_g[:].rearrange("p b n -> p (b n)")
+        quantize(w3_w[:, 0:512], w3_s[:, 0:512], w3_flat[:, 0:2048])
+        quantize(w3_w[:, 512:768], w3_s[:, 512:768], w3_flat[:, 2048:3072])
+
         z_w = [alloc("z_w%d" % b, [P, M], U32) for b in range(HALVES)]
         z_s = [alloc("z_s%d" % b, [P, M], U8) for b in range(HALVES)]
         z_t = [alloc("z_t%d" % i, [P, PACK * P], BF16) for i in range(2)]
         sum_banks = turn_banks + back_banks
 
+        def turn_into(c, t, rows, start, stop):
+            nc.tensor.matmul(sum_banks[c % 4][:, P * t:P * (t + 1)], lhsT=rows, rhs=ident[:], start=start, stop=stop, is_transpose=True)
+
         def sums(c):
-            bank = sum_banks[c % 4]
             for t in range(PACK):
-                nc.tensor.matmul(bank[:, P * t:P * (t + 1)], lhsT=stiff0[:, t, P * c:P * (c + 1)], rhs=ident[:], start=True, stop=False,
-                                 is_transpose=True)
-                nc.tensor.matmul(bank[:, P * t:P * (t + 1)], lhsT=x[:, t, P * c:P * (c + 1)], rhs=ident[:], start=False, stop=True,
-                                 is_transpose=True)
+                turn_into(c, t, stiff0[:, t, P * c:P * (c + 1)], True, False)
+                turn_into(c, t, x_first[t][:, P * c:P * (c + 1)], False, True)
 
         def round_sums(c):
             nc.scalar.copy(out=z_t[c % 2][:].rearrange("m (u p e) -> m u p e", u=2, e=2),
@@ -270,14 +304,15 @@ def tile_list_braille_dot_height_kernel(tc, tab_words, tab_scales, w1, b1, w2_wo
                 o = (c % 2) * 2 * P + u * P
                 nc.tensor.transpose(bank[:, o:o + P], words[:, P * u:P * (u + 1)], ident[:])
 
-        def weave(pair):
-            words = z_g[:].bitcast(F32)[:, 4 * P * pair:4 * P * (pair + 1)]
-            nc.scalar.copy(out=words.rearrange("p (c m u) -> p c m u", c=2, u=2),
+        def weave(pair, dst):
+            nc.scalar.copy(out=dst.bitcast(F32).rearrange("p (c m u) -> p c m u", c=2, u=2),
                            in_=wear_banks[pair % 2][:].rearrange("p (c u m) -> p c m u", c=2, u=2))
 
-        def quantize_z(b, m0, width):
-            quantize(z_w[b][:, m0:m0 + width], z_s[b][:, m0:m0 + width], z_g[:, PACK * m0:PACK * (m0 + width)])
+        def quantize_z(b, m0, width, values):
+            quantize(z_w[b][:, m0:m0 + width], z_s[b][:, m0:m0 + width], values)
 
+        z_first = alloc("z_first", [P, M * PACK], BF16, tag="mag1")
+        pair_cols = 2 * P * PACK
         sums(0)
         sums(1)
         for c in range(M // P):
@@ -286,55 +321,86 @@ def tile_list_braille_dot_height_kernel(tc, tab_words, tab_scales, w1, b1, w2_wo
             round_sums(c)
             words_back(c)
             if c % 2 == 0 and c > 0:
-                weave(c // 2 - 1)
-        weave(M // P // 2 - 1)
+                weave(c // 2 - 1, z_first[:, pair_cols * (c // 2 - 1):pair_cols * (c // 2)])
+        weave(M // P // 2 - 1, z_first[:, M * PACK - pair_cols:M * PACK])
         for h in range(2):
-            quantize_z(0, BANK * h, BANK)
-
-        w3_g = alloc("w3_g", [P, HALVES, N * PACK], BF16)
-        w3_w = alloc("w3_w", [P, HALVES * N], U32)
-        w3_s = alloc("w3_s", [P, HALVES * N], U8)
-        for b in range(HALVES):
-            for c in range(N // P):
-                nc.scalar.copy(out=w3_g[:, b, PACK * P * c:PACK * P * (c + 1)].rearrange("p (c i j) -> p c j i", i=4, j=PACK),
-                               in_=w3_raw[:, b, :, P * c:P * (c + 1)].rearrange("p j (c i) -> p c j i", i=4))
-        w3_flat = w3_g[:].rearrange("p b n -> p (b n)")
-        quantize(w3_w[:, 0:512], w3_s[:, 0:512], w3_flat[:, 0:2048])
-        quantize(w3_w[:, 512:768], w3_s[:, 512:768], w3_flat[:, 2048:3072])
+            quantize_z(0, BANK * h, BANK, z_first[:, PACK * BANK * h:PACK * BANK * (h + 1)])
 
         out_rows = out.rearrange("(c p) m -> p c m", p=P)
 
-        def add_stiff(m0, width):
-            h, c = divmod(m0, BANK)
-            nc.vector.tensor_tensor(z_g[:, PACK * m0:PACK * (m0 + width)].rearrange("p (c i t) -> p c t i", i=4, t=PACK),
-                                    x[:, :, m0:m0 + width].rearrange("p t (c i) -> p c t i", i=4),
-                                    stiff1[h][:, :, c:c + width].rearrange("p t (c i) -> p c t i", i=4), ADD)
+        def open_sum(c):
+            for t in range(PACK):
+                turn_into(c, t, stiff1[c // 4][:, t, P * (c % 4):P * (c % 4 + 1)], t == 0, False)
 
-        def last_product(i):
+        for c in range(4):
+            open_sum(c)
+
+        x_tags = ["mag1", "w1_raw1", "mag0", "z_last0", "z_last0"]
+        z_tags = ["z_last0", "z_last1", "z_last2", "z_last1", "z_last2"]
+        xs = {}
+        zs = {}
+
+        def picks(i):
             m0, width = TAIL[i]
-            two = banks[(2 * i + 2) % 8:(2 * i + 2) % 8 + 2]
-            result = alloc("result%d" % i, [P, N // P, width], F32, tag="lift%d" % (i % RING))
+            xs[i] = alloc("x_last%d" % i, [P, PACK, width], F32, tag=x_tags[i])
+            for t in range(PACK):
+                pick(xs[i][:, t, :], t, m0, width)
+
+        def z_by_transposes(i):
+            m0, width = TAIL[i]
+            zs[i] = alloc("z_last%d" % i, [P, PACK * width], BF16, tag=z_tags[i])
+            for c in range(2):
+                for t in range(PACK):
+                    turn_into(2 * i + c, t, xs[i][:, t, P * c:P * (c + 1)], False, t == PACK - 1)
+            for c in range(2):
+                round_sums(2 * i + c)
+                words_back(2 * i + c)
+                if i == 0:
+                    open_sum(4 + c)
+            weave(i, zs[i][:])
+
+        def z_at_once(i):
+            m0, width = TAIL[i]
+            zs[i] = alloc("z_last%d" % i, [P, PACK * width], BF16, tag=z_tags[i])
+            nc.vector.tensor_tensor(zs[i][:].rearrange("p (m t) -> p m t", t=PACK), xs[i][:].rearrange("p t m -> p m t"),
+                                    stiff1[1][:, :, m0 - BANK:m0 - BANK + width].rearrange("p t m -> p m t"), ADD)
+
+        out_banks = lift_banks + lift_banks + sum_banks[2:4] + sum_banks[0:2]
+
+        def last_passes(chunk, b):
             for c in range(N // P):
+                cols = slice(N * b + P * c, N * b + P * (c + 1))
+                ms = slice(P * chunk, P * (chunk + 1))
+                nc.tensor.matmul_mx(out=out_banks[chunk][:, P * c:P * (c + 1)], lhsT=w3_w[:, cols].bitcast(FP8X4), lhsT_scale=w3_s[:, cols],
+                                    rhs=z_w[b][:, ms].bitcast(FP8X4), rhs_scale=z_s[b][:, ms],
+                                    start=(b == 0 and c == 0), stop=(b == HALVES - 1 and c == N // P - 1))
+
+        def finish(i):
+            m0, width = TAIL[i]
+            quantize_z(1, m0, width, zs[i][:])
+            result = alloc("result%d" % i, [P, N // P, width], F32, tag="lift%d" % ((i + 4) % RING))
+            for k in range(width // P):
+                chunk = m0 // P + k
                 for b in range(HALVES):
-                    cols = slice(N * b + P * c, N * b + P * (c + 1))
-                    nc.tensor.matmul_mx(out=place(two, c, width), lhsT=w3_w[:, cols].bitcast(FP8X4), lhsT_scale=w3_s[:, cols],
-                                        rhs=z_w[b][:, m0:m0 + width].bitcast(FP8X4), rhs_scale=z_s[b][:, m0:m0 + width],
-                                        start=(b == 0), stop=(b == HALVES - 1))
-            for c in range(N // P):
-                nc.scalar.activation(out=result[:, c, :], in_=place(two, c, width), func=ACT.Identity, bias=b3_t[:, c:c + 1])
+                    last_passes(chunk, b)
+                if i == len(TAIL) - 1:
+                    nc.vector.tensor_tensor(result[:], out_banks[chunk][:, 0:N].rearrange("p (c m) -> p c m", m=P),
+                                            b3_t[:].unsqueeze(2).to_broadcast([P, N // P, P]), ADD)
+                else:
+                    for c in range(N // P):
+                        nc.scalar.activation(out=result[:, c, P * k:P * (k + 1)], in_=out_banks[chunk][:, P * c:P * (c + 1)],
+                                             func=ACT.Identity, bias=b3_t[:, c:c + 1])
             nc.sync.dma_start(out=out_rows[:, :, m0:m0 + width], in_=result[:])
 
-        for t in range(PACK):
-            pick(t, *TAIL[0])
-        for i in range(len(TAIL)):
-            ahead = TAIL[i + 1] if i + 1 < len(TAIL) else None
-            if ahead:
-                pick(0, *ahead)
-            add_stiff(*TAIL[i])
-            if ahead:
-                pick(1, *ahead)
-            quantize_z(1, *TAIL[i])
-            if ahead:
-                pick(2, *ahead)
-                pick(3, *ahead)
-            last_product(i)
+        for i in range(3):
+            picks(i)
+            z_by_transposes(i)
+        finish(0)
+        picks(3)
+        finish(1)
+        z_at_once(3)
+        picks(4)
+        finish(2)
+        finish(3)
+        z_at_once(4)
+        finish(4)

@@ -54,6 +54,14 @@ def tile_list_braille_dot_height_kernel(tc, tab_words, tab_scales, w1, b1, w2_wo
         w2_s = alloc("w2_s", [P, H], U8)
         nc.vector.memset(tab_s[:].bitcast(I32), 0)
         nc.vector.memset(w2_s[:].bitcast(I32), 0)
+        CHUNKS = S // P
+        W_ROWS = GROUPS * CHUNKS
+        rows = alloc("rows", [P, P], F32)
+        nc.vector.memset(rows[:], 0.0)
+        seed = alloc("seed", [P, 1], F32)
+        nc.gpsimd.memset(seed[:], 0.0)
+        warm = alloc("warm", [P, 1], F32)
+        nc.scalar.activation(out=warm[:], in_=seed[:], func=ACT.Abs_reciprocal_sqrt, bias=1.0)
 
         tab_w = alloc("tab_w", [P, T], U32)
         tab_src = tab_words[0].rearrange("p n t -> p (n t)").bitcast(I32)
@@ -62,12 +70,18 @@ def tile_list_braille_dot_height_kernel(tc, tab_words, tab_scales, w1, b1, w2_wo
         w1_rows = w1.rearrange("(p j) c -> p j c", j=PACK)
         w1_raw = [[alloc("w1_raw0_%d" % h, [P, PACK, BANK // 2], F32) for h in range(2)]]
 
+        def load_table(c0, c1):
+            nc.sync.dma_start(out=tab_w[:].bitcast(I32)[:, c0:c1], in_=tab_src[:, c0:c1])
+
         nc.sync.dma_start(idx1[:], offs)
-        nc.sync.dma_start(out=tab_w[:].bitcast(I32)[:, 0:T // 2], in_=tab_src[:, 0:T // 2])
+        load_table(0, T // 4)
         for q in range(4):
             nc.sync.dma_start(out=tab_s[32 * q:32 * q + 4, :].bitcast(I32), in_=tab_scales[0, 4 * q:4 * q + 4, :].bitcast(I32))
+        nc.sync.dma_start(out=rows[0:W_ROWS, :], in_=wgs.rearrange("(g s) (c j) -> s g c j", s=GROUP, j=P)[0])
+        load_table(T // 4, 3 * T // 4)
+        nc.sync.dma_start(out=rows[W_ROWS:W_ROWS + H // P, :], in_=b2.rearrange("(c p) -> c p", p=P))
+        load_table(3 * T // 4, T)
         nc.sync.dma_start(out=w2_w[0][:].bitcast(I32), in_=w2_src[:, 0:BANK // 2])
-        nc.sync.dma_start(out=tab_w[:].bitcast(I32)[:, T // 2:T], in_=tab_src[:, T // 2:T])
         for q in range(4):
             nc.sync.dma_start(out=w2_s[32 * q:32 * q + 4, :].bitcast(I32), in_=w2_scales[0, 4 * q:4 * q + 4, :].bitcast(I32))
         for h in range(2):
@@ -90,33 +104,31 @@ def tile_list_braille_dot_height_kernel(tc, tab_words, tab_scales, w1, b1, w2_wo
         with nc.allow_non_contiguous_dma(reason="one bias value a partition"):
             nc.sync.dma_start(out=b3_t[:], in_=b3.rearrange("(c p) -> p c", p=P))
 
-        CHUNKS = S // P
-        W_ROWS = GROUPS * CHUNKS
-        rows = alloc("rows", [P, P], F32)
-        nc.gpsimd.memset(rows[:], 0.0)
-        nc.gpsimd.dma_start(out=rows[0:W_ROWS, :], in_=wgs.rearrange("(g s) (c j) -> s g c j", s=GROUP, j=P)[0])
-        nc.gpsimd.dma_start(out=rows[W_ROWS:W_ROWS + H // P, :], in_=b2.rearrange("(c p) -> c p", p=P))
         ident = alloc("ident", [P, P], F32)
         make_identity(nc, ident[:])
 
-        warm = alloc("warm", [P, 1], F32)
-        nc.scalar.activation(out=warm[:], in_=ident[:, 0:1], func=ACT.Abs_reciprocal_sqrt, bias=1.0)
 
-        pages = [alloc("page%d" % t, [P, T2], F32) for t in range(PACK)]
-        for t in range(PACK):
+        pages = [alloc("page%d" % t, [P, T2], F32) for t in range(2)]
+        for t in range(2):
             nc.vector.memset(pages[t][:].bitcast(I32), 0)
 
         nc.tensor.transpose(back_banks[1][:, 0:P], rows[:], ident[:])
+        pages.append(alloc("page2", [P, T2], F32, tag="rows"))
+        nc.gpsimd.memset(pages[2][:], 0.0)
         inv_wgs = alloc("inv_wgs", [P, W_ROWS], F32)
         b2_t = alloc("b2_t", [P, H // P], F32)
         nc.scalar.copy(out=b2_t[:], in_=back_banks[1][:, W_ROWS:W_ROWS + H // P])
-        nc.vector.reciprocal(out=inv_wgs[:], in_=back_banks[1][:, 0:W_ROWS])
 
         v_s = alloc("v_s", [P, S], U8)
         nc.vector.tensor_copy(out=v_s[:], in_=tab_s[:].indirect(idx1[:]))
-        v_w = [alloc("v_w%d" % h, [P, LOOK], U32) for h in range(S // LOOK)]
-        for h in range(S // LOOK):
+        v_w = []
+
+        def look_up(h, tag):
+            v_w.append(alloc("v_w%d" % h, [P, LOOK], U32, tag=tag))
             nc.vector.tensor_copy(out=v_w[h][:], in_=tab_w[:].indirect(idx1[:, h * LOOK // 16:(h + 1) * LOOK // 16]))
+
+        look_up(0, None)
+        nc.vector.reciprocal(out=inv_wgs[:], in_=back_banks[1][:, 0:W_ROWS])
 
         w1_g = [alloc("w1_g0", [P, PACK * BANK], BF16)]
         w1_w = [alloc("w1_w%d" % b, [P, BANK], U32) for b in range(HALVES)]
@@ -135,7 +147,10 @@ def tile_list_braille_dot_height_kernel(tc, tab_words, tab_scales, w1, b1, w2_wo
             cols = slice(h * BANK // 2, (h + 1) * BANK // 2)
             quantize(w1_w[0][:, cols], w1_s[0][:, cols], w1_g[0][:, h * 2 * BANK:(h + 1) * 2 * BANK])
 
-        stiff1 = [alloc("stiff1_%d" % h, [P, PACK, BANK], F32, tag="w1_raw0_%d" % h) for h in range(2)]
+        look_up(1, "w1_raw0_1")
+        pages.append(alloc("page3", [P, T2], F32, tag="w1_g0"))
+        nc.gpsimd.memset(pages[3][:], 0.0)
+        stiff1 = [alloc("stiff1_%d" % h, [P, PACK, BANK], F32, tag=("w1_raw0_0", None)[h]) for h in range(2)]
         for h in range(2):
             nc.sync.dma_start(out=stiff1[h][:], in_=stiff_rows[1][:, :, BANK * h:BANK * (h + 1)])
 
@@ -335,7 +350,7 @@ def tile_list_braille_dot_height_kernel(tc, tab_words, tab_scales, w1, b1, w2_wo
         for c in range(4):
             open_sum(c)
 
-        x_tags = ["mag1", "w1_raw1", "mag0", "z_last0", "z_last0"]
+        x_tags = [None, "w1_raw1", "mag1", "z_last0", "z_last0"]
         z_tags = ["z_last0", "z_last1", "z_last2", "z_last1", "z_last2"]
         xs = {}
         zs = {}
@@ -349,15 +364,20 @@ def tile_list_braille_dot_height_kernel(tc, tab_words, tab_scales, w1, b1, w2_wo
         def z_by_transposes(i):
             m0, width = TAIL[i]
             zs[i] = alloc("z_last%d" % i, [P, PACK * width], BF16, tag=z_tags[i])
-            for c in range(2):
-                for t in range(PACK):
+            for t in range(PACK):
+                for c in range(2):
                     turn_into(2 * i + c, t, xs[i][:, t, P * c:P * (c + 1)], False, t == PACK - 1)
             for c in range(2):
                 round_sums(2 * i + c)
                 words_back(2 * i + c)
-                if i == 0:
-                    open_sum(4 + c)
             weave(i, zs[i][:])
+
+        def z_by_sum(i):
+            m0, width = TAIL[i]
+            total = alloc("total", [P, PACK, width], F32, tag="mag0")
+            nc.vector.tensor_tensor(total[:], xs[i][:], stiff1[1][:, :, m0 - BANK:m0 - BANK + width], ADD)
+            zs[i] = alloc("z_last%d" % i, [P, PACK * width], BF16, tag=z_tags[i])
+            nc.scalar.copy(out=zs[i][:].rearrange("p (m t) -> p m t", t=PACK), in_=total[:].rearrange("p t m -> p m t"))
 
         def z_at_once(i):
             m0, width = TAIL[i]
@@ -365,36 +385,42 @@ def tile_list_braille_dot_height_kernel(tc, tab_words, tab_scales, w1, b1, w2_wo
             nc.vector.tensor_tensor(zs[i][:].rearrange("p (m t) -> p m t", t=PACK), xs[i][:].rearrange("p t m -> p m t"),
                                     stiff1[1][:, :, m0 - BANK:m0 - BANK + width].rearrange("p t m -> p m t"), ADD)
 
-        out_banks = lift_banks + lift_banks + sum_banks[2:4] + sum_banks[0:2]
+        out_banks = [lift_banks, lift_banks, sum_banks[0:2], sum_banks[2:3], sum_banks[3:4]]
 
-        def last_passes(chunk, b):
-            for c in range(N // P):
-                cols = slice(N * b + P * c, N * b + P * (c + 1))
-                ms = slice(P * chunk, P * (chunk + 1))
-                nc.tensor.matmul_mx(out=out_banks[chunk][:, P * c:P * (c + 1)], lhsT=w3_w[:, cols].bitcast(FP8X4), lhsT_scale=w3_s[:, cols],
-                                    rhs=z_w[b][:, ms].bitcast(FP8X4), rhs_scale=z_s[b][:, ms],
-                                    start=(b == 0 and c == 0), stop=(b == HALVES - 1 and c == N // P - 1))
+        def out_place(i, c):
+            width = TAIL[i][1]
+            h, o = divmod(c * width, BANK)
+            return out_banks[i][h][:, o:o + width]
+
+        def last_passes(i):
+            m0, width = TAIL[i]
+            per = BANK // width
+            for b in range(HALVES):
+                for c in range(N // P):
+                    cols = slice(N * b + P * c, N * b + P * (c + 1))
+                    nc.tensor.matmul_mx(out=out_place(i, c), lhsT=w3_w[:, cols].bitcast(FP8X4), lhsT_scale=w3_s[:, cols],
+                                        rhs=z_w[b][:, m0:m0 + width].bitcast(FP8X4), rhs_scale=z_s[b][:, m0:m0 + width],
+                                        start=(b == 0 and c % per == 0),
+                                        stop=(b == HALVES - 1 and (c % per == per - 1 or c == N // P - 1)))
 
         def finish(i):
             m0, width = TAIL[i]
             quantize_z(1, m0, width, zs[i][:])
             result = alloc("result%d" % i, [P, N // P, width], F32, tag="lift%d" % ((i + 4) % RING))
-            for k in range(width // P):
-                chunk = m0 // P + k
-                for b in range(HALVES):
-                    last_passes(chunk, b)
-                if i == len(TAIL) - 1:
-                    nc.vector.tensor_tensor(result[:], out_banks[chunk][:, 0:N].rearrange("p (c m) -> p c m", m=P),
-                                            b3_t[:].unsqueeze(2).to_broadcast([P, N // P, P]), ADD)
-                else:
-                    for c in range(N // P):
-                        nc.scalar.activation(out=result[:, c, P * k:P * (k + 1)], in_=out_banks[chunk][:, P * c:P * (c + 1)],
-                                             func=ACT.Identity, bias=b3_t[:, c:c + 1])
+            last_passes(i)
+            if i == len(TAIL) - 1:
+                nc.vector.tensor_tensor(result[:], out_banks[i][0][:, 0:N].rearrange("p (c m) -> p c m", m=P),
+                                        b3_t[:].unsqueeze(2).to_broadcast([P, N // P, P]), ADD)
+            else:
+                for c in range(N // P):
+                    nc.scalar.activation(out=result[:, c, :], in_=out_place(i, c), func=ACT.Identity, bias=b3_t[:, c:c + 1])
             nc.sync.dma_start(out=out_rows[:, :, m0:m0 + width], in_=result[:])
 
-        for i in range(3):
+        for i in range(2):
             picks(i)
             z_by_transposes(i)
+        picks(2)
+        z_by_sum(2)
         finish(0)
         picks(3)
         finish(1)

from contextlib import ExitStack

import concourse.mybir as mybir
from concourse.masks import make_identity

K, H, N, T, S, T2, M = 512, 1024, 384, 4096, 1024, 2048, 1024
FLOPS = 2 * K * H * S * 2 + 2 * H * N * M

F32 = mybir.dt.float32
BF16 = mybir.dt.bfloat16
I32 = mybir.dt.int32
U32 = mybir.dt.uint32
U16 = mybir.dt.uint16
U8 = mybir.dt.uint8
FP8X4 = mybir.dt.float8_e4m3fn_x4
FP4X4 = mybir.dt.float4_e2m1fn_x4
ACT = mybir.ActivationFunctionType
MULT = mybir.AluOpType.mult
ADD = mybir.AluOpType.add

P = 128
PACK = 4
HALVES = H // (P * PACK)
GROUPS = 8
GROUP = 16
BANK = 512
LOOK = 512

STEPS = [(0, 0, 128), (0, 128, 128), (0, 256, 256), (0, 512, 256), (0, 768, 256),
         (1, 0, 256), (1, 256, 256), (1, 512, 256), (1, 768, 256)]
TAIL = [(0, 256), (256, 256), (512, 256), (768, 128), (896, 128)]
RING = 5


def tile_list_braille_dot_height_kernel(tc, tab_words, tab_scales, w1, b1, w2_words, w2_scales, b2, wgs, wgt,
                                                   stiff, w3, b3, offs, offs2, offs3, out):
    nc = tc.nc
    with ExitStack() as ctx:
        lists = ctx.enter_context(tc.tile_pool(name="lists", bufs=1))
        keep = ctx.enter_context(tc.tile_pool(name="keep", bufs=1))
        psum = ctx.enter_context(tc.psum_pool(name="psum", bufs=1))

        def alloc(name, shape, dtype, tag=None):
            return keep.tile(shape, dtype, name=name, tag=tag or name, align_bytes=64)

        banks = [psum.tile([P, BANK], F32, name="bank%d" % i) for i in range(8)]
        wear_banks, lift_banks, turn_banks, back_banks = banks[0:2], banks[2:4], banks[4:6], banks[6:8]

        idx1 = lists.tile([P, S // 16], U16, name="idx1")
        idx2 = lists.tile([P, S // 16], U16, name="idx2")
        idx3 = lists.tile([P, M // 16], U16, name="idx3")

        tab_s = alloc("tab_s", [P, T], U8)
        w2_s = alloc("w2_s", [P, H], U8)
        nc.vector.memset(tab_s[:].bitcast(I32), 0)
        nc.vector.memset(w2_s[:].bitcast(I32), 0)
        CHUNKS = S // P
        W_ROWS = GROUPS * CHUNKS
        rows = alloc("rows", [P, P], F32)
        nc.vector.memset(rows[:], 0.0)
        seed = alloc("seed", [P, 1], F32)
        nc.gpsimd.memset(seed[:], 0.0)
        warm = alloc("warm", [P, 1], F32)
        nc.scalar.activation(out=warm[:], in_=seed[:], func=ACT.Abs_reciprocal_sqrt, bias=1.0)

        tab_w = alloc("tab_w", [P, T], U32)
        tab_src = tab_words[0].rearrange("p n t -> p (n t)").bitcast(I32)
        w2_src = w2_words[0].bitcast(I32)
        w2_w = [alloc("w2_w%d" % b, [P, 2 * BANK], U8) for b in range(HALVES)]
        w1_rows = w1.rearrange("(p j) c -> p j c", j=PACK)
        w1_raw = [[alloc("w1_raw0_%d" % h, [P, PACK, BANK // 2], F32) for h in range(2)]]

        def load_table(c0, c1):
            nc.sync.dma_start(out=tab_w[:].bitcast(I32)[:, c0:c1], in_=tab_src[:, c0:c1])

        nc.sync.dma_start(idx1[:], offs)
        load_table(0, T // 4)
        for q in range(4):
            nc.sync.dma_start(out=tab_s[32 * q:32 * q + 4, :].bitcast(I32), in_=tab_scales[0, 4 * q:4 * q + 4, :].bitcast(I32))
        nc.sync.dma_start(out=rows[0:W_ROWS, :], in_=wgs.rearrange("(g s) (c j) -> s g c j", s=GROUP, j=P)[0])
        load_table(T // 4, 3 * T // 4)
        nc.sync.dma_start(out=rows[W_ROWS:W_ROWS + H // P, :], in_=b2.rearrange("(c p) -> c p", p=P))
        load_table(3 * T // 4, T)
        nc.sync.dma_start(out=w2_w[0][:].bitcast(I32), in_=w2_src[:, 0:BANK // 2])
        for q in range(4):
            nc.sync.dma_start(out=w2_s[32 * q:32 * q + 4, :].bitcast(I32), in_=w2_scales[0, 4 * q:4 * q + 4, :].bitcast(I32))
        for h in range(2):
            nc.sync.dma_start(out=w1_raw[0][h][:], in_=w1_rows[:, :, h * BANK // 2:(h + 1) * BANK // 2])
        nc.sync.dma_start(idx2[:], offs2)
        b1_t = alloc("b1_t", [P, HALVES, PACK], F32)
        nc.sync.dma_start(out=b1_t[:], in_=b1.rearrange("(b p t) -> p b t", b=HALVES, t=PACK))
        nc.sync.dma_start(out=w2_w[1][:].bitcast(I32), in_=w2_src[:, BANK // 2:BANK])
        w1_raw.append([alloc("w1_raw1", [P, PACK, BANK], F32)])
        nc.sync.dma_start(out=w1_raw[1][0][:], in_=w1_rows[:, :, BANK:2 * BANK])
        nc.sync.dma_start(idx3[:], offs3)
        wgt_t = alloc("wgt_t", [P, M], F32)
        nc.sync.dma_start(out=wgt_t[:], in_=wgt)
        w3_raw = alloc("w3_raw", [P, HALVES, PACK, N], F32)
        nc.sync.dma_start(out=w3_raw[:].rearrange("p b j n -> p b (j n)"), in_=w3.rearrange("(b p j) n -> p b (j n)", b=HALVES, j=PACK))
        stiff_rows = stiff.rearrange("(b p t) m -> b p t m", b=HALVES, t=PACK)
        stiff0 = alloc("stiff0", [P, PACK, M], F32)
        nc.sync.dma_start(out=stiff0[:], in_=stiff_rows[0])
        b3_t = alloc("b3_t", [P, N // P], F32)
        with nc.allow_non_contiguous_dma(reason="one bias value a partition"):
            nc.sync.dma_start(out=b3_t[:], in_=b3.rearrange("(c p) -> p c", p=P))

        ident = alloc("ident", [P, P], F32)
        make_identity(nc, ident[:])


        pages = [alloc("page%d" % t, [P, T2], F32) for t in range(2)]
        for t in range(2):
            nc.vector.memset(pages[t][:].bitcast(I32), 0)

        nc.tensor.transpose(back_banks[1][:, 0:P], rows[:], ident[:])
        pages.append(alloc("page2", [P, T2], F32, tag="rows"))
        nc.gpsimd.memset(pages[2][:], 0.0)
        inv_wgs = alloc("inv_wgs", [P, W_ROWS], F32)
        b2_t = alloc("b2_t", [P, H // P], F32)
        nc.scalar.copy(out=b2_t[:], in_=back_banks[1][:, W_ROWS:W_ROWS + H // P])

        v_s = alloc("v_s", [P, S], U8)
        nc.vector.tensor_copy(out=v_s[:], in_=tab_s[:].indirect(idx1[:]))
        v_w = []

        def look_up(h, tag):
            v_w.append(alloc("v_w%d" % h, [P, LOOK], U32, tag=tag))
            nc.vector.tensor_copy(out=v_w[h][:], in_=tab_w[:].indirect(idx1[:, h * LOOK // 16:(h + 1) * LOOK // 16]))

        look_up(0, None)
        nc.vector.reciprocal(out=inv_wgs[:], in_=back_banks[1][:, 0:W_ROWS])

        w1_g = [alloc("w1_g0", [P, PACK * BANK], BF16)]
        w1_w = [alloc("w1_w%d" % b, [P, BANK], U32) for b in range(HALVES)]
        w1_s = [alloc("w1_s%d" % b, [P, BANK], U8) for b in range(HALVES)]

        def round_w1(copy, b, src, m0, count):
            copy(out=w1_g[b][:].rearrange("p (t m j) -> p m t j", t=PACK, j=PACK)[:, m0:m0 + count],
                 in_=src.rearrange("p j (m t) -> p m t j", t=PACK))

        def quantize(words, scales, values):
            nc.vector.quantize_mx(out=words.bitcast(FP8X4), scales=scales, in_=values)

        for h in range(2):
            round_w1(nc.vector.tensor_copy, 0, w1_raw[0][h][:], h * P // 2, P // 2)
        for h in range(2):
            cols = slice(h * BANK // 2, (h + 1) * BANK // 2)
            quantize(w1_w[0][:, cols], w1_s[0][:, cols], w1_g[0][:, h * 2 * BANK:(h + 1) * 2 * BANK])

        look_up(1, "w1_raw0_1")
        pages.append(alloc("page3", [P, T2], F32, tag="w1_g0"))
        nc.gpsimd.memset(pages[3][:], 0.0)
        stiff1 = [alloc("stiff1_%d" % h, [P, PACK, BANK], F32, tag=("w1_raw0_0", None)[h]) for h in range(2)]
        for h in range(2):
            nc.sync.dma_start(out=stiff1[h][:], in_=stiff_rows[1][:, :, BANK * h:BANK * (h + 1)])

        mags = [alloc("mag%d" % i, [P, PACK, 256], F32) for i in range(2)]
        root_pair = [alloc("root%d" % i, [P, PACK, P], F32) for i in range(2)]
        root_last = alloc("root_last", [P, PACK, P], F32)

        def root(u, k):
            chunk = STEPS[u][1] // P + k
            return root_last if (STEPS[u][0], chunk) == (0, CHUNKS - 1) else root_pair[chunk % 2]

        damp = {}
        lift = {}

        def place(banks2, i, width):
            return banks2[i // 2][:, (i % 2) * width:(i % 2 + 1) * width]

        def block(banks2, u, k, i):
            per = PACK * (STEPS[u][2] // P) // 2
            h, c = divmod(PACK * k + i, per)
            return banks2[h][:, P * c:P * (c + 1)]

        def moving(j0, width):
            h, c = divmod(j0, LOOK)
            return v_w[h][:, c:c + width].bitcast(FP8X4), v_s[:, j0:j0 + width]

        def wear_products(u):
            b, j0, width = STEPS[u]
            rhs, rhs_s = moving(j0, width)
            for c in range(PACK):
                nc.tensor.matmul_mx(out=place(wear_banks, c, width), lhsT=w2_w[b][:, 2 * P * c:2 * P * (c + 1)].bitcast(FP4X4),
                                    lhsT_scale=w2_s[:, BANK * b + P * c:BANK * b + P * (c + 1)], rhs=rhs, rhs_scale=rhs_s,
                                    start=True, stop=True)

        def lift_products(u):
            b, j0, width = STEPS[u]
            rhs, rhs_s = moving(j0, width)
            for t in range(PACK):
                nc.tensor.matmul_mx(out=place(lift_banks, t, width), lhsT=w1_w[b][:, P * t:P * (t + 1)].bitcast(FP8X4),
                                    lhsT_scale=w1_s[b][:, P * t:P * (t + 1)], rhs=rhs, rhs_scale=rhs_s, start=True, stop=True)

        def magnitudes(u):
            b, j0, width = STEPS[u]
            for c in range(PACK):
                nc.scalar.activation(out=mags[u % 2][:, c, 0:width], in_=place(wear_banks, c, width), func=ACT.Abs,
                                     bias=b2_t[:, PACK * b + c:PACK * b + c + 1])

        def turn(u, k):
            for c in range(PACK):
                nc.tensor.transpose(block(turn_banks, u, k, c), mags[u % 2][:, c, P * k:P * (k + 1)], ident[:])

        def inverse_roots(u, k):
            chunk = STEPS[u][1] // P + k
            for g in range(GROUPS):
                col = inv_wgs[:, g * CHUNKS + chunk:g * CHUNKS + chunk + 1]
                run = block(turn_banks, u, k, g // 2)[:, 64 * (g % 2):64 * (g % 2 + 1)]
                nc.scalar.activation(out=root(u, k)[:, :, GROUP * g:GROUP * (g + 1)], in_=run.rearrange("j (s t) -> j t s", t=PACK),
                                     func=ACT.Abs_reciprocal_sqrt, bias=col, scale=col)

        def turn_back(u, k):
            for t in range(PACK):
                nc.tensor.transpose(block(back_banks, u, k, t), root(u, k)[:, t, :], ident[:])

        def squares(u, k):
            width = STEPS[u][2]
            if k == 0:
                damp[u] = alloc("damp%d" % u, [P, PACK, width], F32, tag="damp%d" % (u % RING))
            if width == P:
                for h in range(2):
                    nc.scalar.activation(out=damp[u][:, 2 * h:2 * h + 2, :], in_=back_banks[h][:, 0:2 * P].rearrange("p (t j) -> p t j", t=2),
                                         func=ACT.Square)
            else:
                nc.scalar.activation(out=damp[u][:, :, P * k:P * (k + 1)], in_=back_banks[k][:].rearrange("p (t j) -> p t j", t=PACK),
                                     func=ACT.Square)

        def lifts(u):
            b, j0, width = STEPS[u]
            lift[u] = alloc("lift%d" % u, [P, PACK, width], F32, tag="lift%d" % (u % RING))
            for t in range(PACK):
                nc.scalar.activation(out=lift[u][:, t, :], in_=place(lift_banks, t, width), func=ACT.Identity, bias=b1_t[:, b, t:t + 1])

        def put(u, c0, width):
            j0 = STEPS[u][1] + c0
            cols = idx2[:, j0 // 16:(j0 + width) // 16]
            for t in range(PACK):
                nc.vector.tensor_tensor(pages[t][:].indirect(cols), lift[u][:, t, c0:c0 + width], damp[u][:, t, c0:c0 + width], MULT)

        def pick(dst, t, m0, width):
            nc.vector.tensor_tensor(dst, pages[t][:].indirect(idx3[:, m0 // 16:(m0 + width) // 16]), wgt_t[:, m0:m0 + width], MULT)

        w3_w = alloc("w3_w", [P, HALVES * N], U32)
        w3_s = alloc("w3_s", [P, HALVES * N], U8)
        x_first = []

        def between_halves():
            w1_g.append(alloc("w1_g1", [P, PACK * BANK], BF16, tag="root_last"))
            for m0 in range(0, P, 32):
                round_w1(nc.scalar.copy, 1, w1_raw[1][0][:, :, PACK * m0:PACK * (m0 + 32)], m0, 32)
            quantize(w1_w[1][:], w1_s[1][:], w1_g[1][:])
            for t in range(PACK):
                x_first.append(alloc("x_first%d" % t, [P, M], F32, tag="root_last" if t == 0 else None))
                pick(x_first[t][:], t, 0, M)

        FIRST = [u for u in range(len(STEPS)) if STEPS[u][0] == 0]
        LATE = [len(FIRST), len(FIRST) + 1]
        wear_products(0)
        magnitudes(0)
        for u in range(len(STEPS)):
            width = STEPS[u][2]
            last = width // P - 1
            for k in range(last + 1):
                turn(u, k)
            if u not in LATE:
                lift_products(u)
            for k in range(last + 1):
                inverse_roots(u, k)
                turn_back(u, k)
                if k == 0 and u not in LATE:
                    lifts(u)
                if k == last and u + 1 < len(STEPS):
                    wear_products(u + 1)
                    magnitudes(u + 1)
                squares(u, k)
                if u in FIRST:
                    put(u, P * k, P)
            if u == FIRST[-1]:
                between_halves()
            elif u == LATE[-1]:
                for v in LATE:
                    lift_products(v)
                    lifts(v)
                    put(v, 0, width)
            elif u > LATE[-1]:
                put(u, 0, width)

        w3_g = alloc("w3_g", [P, HALVES, N * PACK], BF16, tag="w1_raw1")
        for b in range(HALVES):
            for c in range(N // P):
                nc.scalar.copy(out=w3_g[:, b, PACK * P * c:PACK * P * (c + 1)].rearrange("p (n j) -> p n j", j=PACK),
                               in_=w3_raw[:, b, :, P * c:P * (c + 1)].rearrange("p j n -> p n j"))
        w3_flat = w3_g[:].rearrange("p b n -> p (b n)")
        quantize(w3_w[:, 0:512], w3_s[:, 0:512], w3_flat[:, 0:2048])
        quantize(w3_w[:, 512:768], w3_s[:, 512:768], w3_flat[:, 2048:3072])

        z_w = [alloc("z_w%d" % b, [P, M], U32) for b in range(HALVES)]
        z_s = [alloc("z_s%d" % b, [P, M], U8) for b in range(HALVES)]
        z_t = [alloc("z_t%d" % i, [P, PACK * P], BF16) for i in range(2)]
        sum_banks = turn_banks + back_banks

        def turn_into(c, t, rows, start, stop):
            nc.tensor.matmul(sum_banks[c % 4][:, P * t:P * (t + 1)], lhsT=rows, rhs=ident[:], start=start, stop=stop, is_transpose=True)

        def sums(c):
            for t in range(PACK):
                turn_into(c, t, stiff0[:, t, P * c:P * (c + 1)], True, False)
                turn_into(c, t, x_first[t][:, P * c:P * (c + 1)], False, True)

        def round_sums(c):
            nc.scalar.copy(out=z_t[c % 2][:].rearrange("m (u p e) -> m u p e", u=2, e=2),
                           in_=sum_banks[c % 4][:].rearrange("m (u e p) -> m u p e", u=2, e=2))

        def words_back(c):
            words = z_t[c % 2][:].bitcast(F32)
            bank = wear_banks[c // 2 % 2]
            for u in range(2):
                o = (c % 2) * 2 * P + u * P
                nc.tensor.transpose(bank[:, o:o + P], words[:, P * u:P * (u + 1)], ident[:])

        def weave(pair, dst):
            nc.scalar.copy(out=dst.bitcast(F32).rearrange("p (c m u) -> p c m u", c=2, u=2),
                           in_=wear_banks[pair % 2][:].rearrange("p (c u m) -> p c m u", c=2, u=2))

        def quantize_z(b, m0, width, values):
            quantize(z_w[b][:, m0:m0 + width], z_s[b][:, m0:m0 + width], values)

        z_first = alloc("z_first", [P, M * PACK], BF16, tag="mag1")
        pair_cols = 2 * P * PACK
        sums(0)
        sums(1)
        for c in range(M // P):
            if c + 2 < M // P:
                sums(c + 2)
            round_sums(c)
            words_back(c)
            if c % 2 == 0 and c > 0:
                weave(c // 2 - 1, z_first[:, pair_cols * (c // 2 - 1):pair_cols * (c // 2)])
        weave(M // P // 2 - 1, z_first[:, M * PACK - pair_cols:M * PACK])
        for h in range(2):
            quantize_z(0, BANK * h, BANK, z_first[:, PACK * BANK * h:PACK * BANK * (h + 1)])

        out_rows = out.rearrange("(c p) m -> p c m", p=P)

        def open_sum(c):
            for t in range(PACK):
                turn_into(c, t, stiff1[c // 4][:, t, P * (c % 4):P * (c % 4 + 1)], t == 0, False)

        for c in range(4):
            open_sum(c)

        x_tags = [None, "w1_raw1", "mag1", "z_last0", "z_last0"]
        z_tags = ["z_last0", "z_last1", "z_last2", "z_last1", "z_last2"]
        xs = {}
        zs = {}

        def picks(i):
            m0, width = TAIL[i]
            xs[i] = alloc("x_last%d" % i, [P, PACK, width], F32, tag=x_tags[i])
            for t in range(PACK):
                pick(xs[i][:, t, :], t, m0, width)

        def z_by_transposes(i):
            m0, width = TAIL[i]
            zs[i] = alloc("z_last%d" % i, [P, PACK * width], BF16, tag=z_tags[i])
            for t in range(PACK):
                for c in range(2):
                    turn_into(2 * i + c, t, xs[i][:, t, P * c:P * (c + 1)], False, t == PACK - 1)
            for c in range(2):
                round_sums(2 * i + c)
                words_back(2 * i + c)
            weave(i, zs[i][:])

        def z_by_sum(i):
            m0, width = TAIL[i]
            total = alloc("total", [P, PACK, width], F32, tag="mag0")
            nc.vector.tensor_tensor(total[:], xs[i][:], stiff1[1][:, :, m0 - BANK:m0 - BANK + width], ADD)
            zs[i] = alloc("z_last%d" % i, [P, PACK * width], BF16, tag=z_tags[i])
            nc.scalar.copy(out=zs[i][:].rearrange("p (m t) -> p m t", t=PACK), in_=total[:].rearrange("p t m -> p m t"))

        def z_at_once(i):
            m0, width = TAIL[i]
            zs[i] = alloc("z_last%d" % i, [P, PACK * width], BF16, tag=z_tags[i])
            nc.vector.tensor_tensor(zs[i][:].rearrange("p (m t) -> p m t", t=PACK), xs[i][:].rearrange("p t m -> p m t"),
                                    stiff1[1][:, :, m0 - BANK:m0 - BANK + width].rearrange("p t m -> p m t"), ADD)

        out_banks = [lift_banks, lift_banks, sum_banks[0:2], sum_banks[2:3], sum_banks[3:4]]

        def out_place(i, c):
            width = TAIL[i][1]
            h, o = divmod(c * width, BANK)
            return out_banks[i][h][:, o:o + width]

        def last_passes(i):
            m0, width = TAIL[i]
            per = BANK // width
            for b in range(HALVES):
                for c in range(N // P):
                    cols = slice(N * b + P * c, N * b + P * (c + 1))
                    nc.tensor.matmul_mx(out=out_place(i, c), lhsT=w3_w[:, cols].bitcast(FP8X4), lhsT_scale=w3_s[:, cols],
                                        rhs=z_w[b][:, m0:m0 + width].bitcast(FP8X4), rhs_scale=z_s[b][:, m0:m0 + width],
                                        start=(b == 0 and c % per == 0),
                                        stop=(b == HALVES - 1 and (c % per == per - 1 or c == N // P - 1)))

        def finish(i):
            m0, width = TAIL[i]
            quantize_z(1, m0, width, zs[i][:])
            result = alloc("result%d" % i, [P, N // P, width], F32, tag="lift%d" % ((i + 4) % RING))
            last_passes(i)
            if i == len(TAIL) - 1:
                nc.vector.tensor_tensor(result[:], out_banks[i][0][:, 0:N].rearrange("p (c m) -> p c m", m=P),
                                        b3_t[:].unsqueeze(2).to_broadcast([P, N // P, P]), ADD)
            else:
                for c in range(N // P):
                    nc.scalar.activation(out=result[:, c, :], in_=out_place(i, c), func=ACT.Identity, bias=b3_t[:, c:c + 1])
            nc.sync.dma_start(out=out_rows[:, :, m0:m0 + width], in_=result[:])

        for i in range(2):
            picks(i)
            z_by_transposes(i)
        picks(2)
        z_by_sum(2)
        finish(0)
        picks(3)
        finish(1)
        z_at_once(3)
        picks(4)
        finish(2)
        finish(3)
        z_at_once(4)
        finish(4)
